import numpy as np
CORES = [0,1,2,3]
N = 4
T, K = 256, 2
ROUTE = [[[2,1],[1,0],[2,0],[0,3],[3,1],[3,2],[3,1],[0,2],[1,0],[1,2],[3,0],[0,3],[0,1],[3,2],[2,3],[2,1],[3,2],[3,0],[3,2],[0,3],[1,3],[0,2],[3,0],[1,2],[3,2],[3,0],[3,0],[2,3],[1,3],[2,0],[1,2],[0,1],[2,0],[1,2],[0,2],[0,3],[3,1],[1,0],[1,2],[1,2],[3,1],[1,0],[0,3],[2,3],[2,0],[0,3],[0,1],[1,2],[1,3],[1,3],[1,2],[2,1],[1,0],[3,1],[3,0],[0,2],[3,0],[1,0],[0,2],[3,2],[0,1],[2,0],[1,3],[3,2],[3,0],[3,1],[3,0],[0,2],[0,1],[2,3],[1,3],[2,1],[2,1],[0,1],[2,0],[0,2],[2,0],[0,1],[2,1],[1,2],[0,1],[3,2],[3,2],[1,0],[0,1],[1,2],[3,1],[3,2],[0,2],[2,1],[2,0],[3,2],[2,3],[3,0],[3,2],[1,0],[3,2],[0,1],[2,0],[3,2],[2,3],[0,1],[0,2],[1,2],[2,0],[0,2],[0,2],[2,3],[0,3],[2,3],[1,2],[2,0],[0,3],[3,2],[1,3],[3,0],[2,1],[0,2],[0,1],[2,1],[1,3],[1,2],[3,0],[2,3],[1,2],[0,1],[1,0],[0,3],[1,0],[0,1],[1,0],[2,1],[2,1],[0,1],[3,1],[2,1],[0,2],[2,3],[3,2],[3,0],[2,1],[0,3],[2,1],[1,2],[2,3],[3,2],[1,3],[0,3],[0,3],[2,3],[3,1],[0,1],[3,0],[3,2],[1,0],[1,2],[3,2],[2,0],[2,3],[2,3],[0,2],[1,0],[2,1],[2,0],[2,0],[3,1],[0,1],[0,1],[2,3],[3,1],[1,0],[0,2],[3,0],[2,1],[3,2],[2,3],[0,3],[0,1],[3,1],[2,0],[1,0],[3,0],[3,1],[1,3],[3,2],[1,0],[2,3],[0,2],[3,2],[0,3],[1,3],[0,1],[2,0],[2,0],[3,2],[3,2],[1,2],[1,0],[1,0],[1,3],[0,3],[0,1],[1,3],[3,0],[0,2],[3,2],[2,1],[2,1],[2,0],[3,1],[3,2],[2,3],[2,1],[0,3],[0,1],[0,1],[1,2],[1,2],[2,0],[3,0],[3,1],[0,3],[1,2],[2,3],[0,2],[3,2],[3,1],[2,3],[1,0],[1,0],[3,0],[1,0],[1,0],[0,1],[3,0],[3,2],[2,0],[3,0],[1,3],[1,0],[3,1],[0,2],[0,2],[3,2],[0,3],[3,0],[3,2],[0,3],[2,0],[2,1],[2,1],[0,1],[0,1],[2,0],[3,1],[2,1]],[[3,1],[3,0],[1,2],[0,2],[2,3],[1,2],[0,2],[2,0],[1,3],[0,3],[0,3],[3,1],[3,1],[2,1],[3,2],[3,2],[0,3],[1,2],[1,3],[0,2],[3,0],[2,1],[0,2],[0,1],[0,1],[0,1],[1,3],[3,2],[0,2],[2,0],[2,1],[3,2],[0,1],[1,3],[3,1],[0,2],[0,1],[2,1],[3,2],[1,0],[1,3],[0,3],[2,1],[2,0],[0,3],[0,3],[2,3],[2,3],[3,0],[3,0],[2,3],[1,2],[3,0],[0,2],[3,2],[0,1],[3,1],[3,2],[0,2],[2,1],[3,0],[3,0],[2,3],[0,1],[1,0],[2,0],[0,2],[2,1],[2,1],[3,0],[0,1],[0,1],[1,0],[3,1],[1,2],[3,2],[3,1],[0,1],[3,2],[2,0],[3,1],[2,3],[2,3],[2,0],[3,2],[0,2],[2,0],[0,1],[1,2],[3,2],[2,1],[0,1],[3,2],[0,3],[3,0],[2,3],[2,3],[0,1],[1,0],[3,2],[0,3],[0,2],[2,3],[2,1],[3,0],[2,1],[2,1],[3,2],[1,0],[1,0],[1,2],[1,3],[3,1],[0,2],[3,1],[1,2],[2,0],[1,2],[3,0],[2,3],[1,2],[3,1],[3,1],[1,2],[0,1],[1,0],[2,1],[0,3],[1,3],[0,3],[2,1],[2,3],[2,0],[3,1],[0,2],[0,1],[0,2],[3,0],[2,1],[0,2],[1,0],[0,3],[3,0],[0,3],[1,3],[2,1],[0,3],[3,1],[3,0],[0,3],[2,0],[1,3],[3,2],[0,2],[0,2],[2,0],[0,2],[1,3],[0,3],[3,2],[0,2],[0,3],[2,3],[0,2],[0,2],[3,2],[2,3],[3,1],[2,1],[3,1],[3,2],[0,3],[1,3],[0,3],[3,0],[3,2],[1,0],[2,3],[1,2],[0,2],[3,0],[2,0],[3,1],[0,2],[2,3],[3,0],[1,0],[0,3],[2,0],[0,1],[2,1],[0,2],[3,0],[1,0],[0,1],[2,1],[1,0],[2,3],[1,0],[1,2],[1,3],[3,1],[3,1],[0,1],[2,0],[1,2],[0,2],[2,0],[2,1],[2,3],[2,1],[3,0],[0,3],[3,2],[2,3],[3,1],[3,1],[2,1],[3,0],[2,0],[1,2],[0,2],[1,3],[2,1],[1,2],[2,3],[2,3],[1,3],[1,3],[2,1],[3,1],[1,3],[2,3],[0,2],[2,1],[0,3],[3,1],[3,0],[2,3],[3,2],[2,1],[3,1],[3,1],[1,2],[0,3],[1,2],[0,2],[3,1],[2,1],[1,3],[1,3],[3,1],[0,3],[0,2],[2,0],[0,2]],[[3,1],[2,1],[0,2],[3,2],[3,2],[3,0],[2,3],[3,1],[3,0],[3,0],[0,2],[3,0],[3,2],[0,3],[2,0],[0,2],[1,3],[1,3],[3,2],[2,1],[3,1],[1,2],[3,0],[1,0],[0,1],[3,2],[1,0],[1,2],[0,2],[3,2],[3,2],[0,3],[1,2],[0,3],[0,2],[0,1],[3,0],[0,2],[2,1],[1,0],[1,3],[1,3],[2,1],[2,0],[0,3],[0,1],[1,3],[1,0],[0,1],[3,2],[2,3],[2,3],[0,1],[0,2],[3,1],[2,1],[3,0],[3,2],[3,1],[1,2],[2,1],[0,3],[0,1],[2,3],[3,1],[0,3],[1,3],[1,2],[1,0],[2,1],[3,1],[1,2],[0,1],[3,0],[1,2],[0,2],[2,1],[0,3],[0,1],[1,0],[2,3],[3,1],[2,3],[3,0],[2,1],[3,0],[2,0],[1,2],[2,0],[0,3],[3,1],[3,0],[3,0],[1,0],[2,0],[1,2],[3,2],[3,0],[3,0],[1,3],[3,1],[2,0],[1,2],[2,3],[0,2],[3,1],[1,0],[2,1],[3,0],[2,3],[0,3],[0,2],[2,3],[3,0],[0,1],[3,2],[3,2],[0,1],[2,1],[2,0],[1,3],[2,1],[2,0],[0,2],[1,2],[1,2],[1,3],[3,2],[2,1],[1,0],[0,1],[2,0],[1,2],[0,1],[3,2],[0,3],[2,1],[2,0],[0,3],[2,3],[3,0],[3,0],[3,1],[2,0],[2,0],[1,3],[1,0],[1,0],[3,0],[1,2],[0,2],[0,1],[1,3],[2,1],[1,2],[2,3],[3,1],[3,1],[3,2],[0,3],[1,3],[2,3],[3,1],[3,2],[2,1],[1,2],[2,0],[2,1],[3,2],[1,2],[0,3],[3,1],[2,3],[1,0],[0,2],[3,1],[1,0],[2,3],[0,2],[1,3],[2,0],[3,0],[0,2],[2,0],[3,2],[2,3],[2,1],[3,1],[0,1],[1,2],[0,3],[3,0],[0,3],[0,2],[2,3],[0,3],[0,2],[3,1],[3,1],[2,3],[0,1],[2,1],[3,0],[1,0],[2,1],[2,0],[2,1],[3,1],[2,1],[3,1],[0,1],[0,1],[0,1],[0,3],[2,1],[2,1],[1,0],[2,3],[2,3],[0,2],[2,1],[0,3],[3,1],[3,0],[3,0],[3,0],[1,2],[2,1],[2,0],[1,2],[3,2],[1,0],[3,1],[3,1],[0,3],[0,2],[1,0],[1,2],[0,2],[1,3],[0,2],[0,3],[3,1],[3,1],[0,2],[1,3],[0,1],[2,0],[0,1],[2,0],[0,2],[1,2],[3,0],[3,1],[2,0],[0,2]],[[1,2],[2,0],[2,0],[2,0],[0,1],[0,2],[1,3],[2,1],[2,0],[3,2],[1,3],[3,1],[0,1],[1,3],[1,0],[2,3],[1,2],[0,3],[1,3],[0,3],[1,0],[3,1],[0,3],[3,0],[3,2],[2,1],[1,3],[3,0],[2,3],[1,0],[1,2],[1,3],[3,2],[3,2],[3,1],[3,0],[0,2],[1,0],[1,3],[2,3],[0,2],[0,2],[3,2],[1,2],[0,3],[2,1],[0,3],[3,1],[1,0],[3,2],[1,0],[1,0],[0,2],[3,0],[2,0],[1,0],[2,0],[1,0],[1,2],[3,1],[2,0],[2,3],[2,3],[3,1],[3,1],[2,3],[3,2],[1,2],[3,1],[2,3],[3,1],[0,3],[0,3],[2,0],[3,1],[1,2],[1,3],[2,3],[0,1],[1,2],[2,0],[3,0],[3,2],[1,2],[1,3],[3,0],[3,1],[0,1],[2,1],[2,1],[1,0],[1,2],[0,3],[0,1],[1,3],[1,2],[2,1],[2,3],[1,3],[3,0],[2,0],[1,0],[0,2],[0,2],[1,0],[3,0],[1,0],[2,3],[0,1],[2,1],[1,3],[2,3],[2,1],[3,0],[1,0],[3,1],[1,3],[2,1],[3,1],[2,3],[2,1],[1,0],[1,0],[2,0],[1,2],[3,1],[3,2],[2,1],[3,1],[3,0],[3,2],[0,1],[2,1],[1,0],[0,1],[1,0],[0,1],[2,0],[1,2],[2,0],[1,3],[1,2],[1,0],[3,0],[3,0],[0,2],[0,1],[0,3],[0,1],[2,0],[2,0],[0,1],[0,2],[0,2],[0,3],[2,0],[0,1],[0,2],[2,0],[1,2],[1,2],[2,3],[1,3],[1,2],[0,3],[1,3],[1,0],[2,1],[0,3],[3,0],[0,1],[0,3],[1,3],[1,2],[1,2],[3,1],[3,1],[3,1],[0,1],[1,3],[3,0],[3,0],[3,0],[3,1],[1,2],[3,1],[2,1],[1,0],[2,0],[0,1],[1,3],[1,0],[0,1],[0,2],[2,3],[3,1],[1,2],[1,0],[0,2],[1,2],[0,3],[1,2],[0,1],[0,3],[3,1],[0,3],[1,3],[3,2],[2,3],[1,2],[1,0],[2,1],[0,1],[1,0],[2,3],[0,1],[1,0],[3,1],[2,1],[3,2],[0,2],[1,3],[2,1],[3,1],[2,3],[2,3],[1,2],[0,2],[1,2],[0,3],[1,3],[3,0],[2,0],[3,2],[1,2],[1,0],[3,1],[0,3],[0,3],[0,1],[3,0],[1,0],[2,0],[2,3],[1,0],[3,2],[1,3],[0,1],[1,3],[1,2],[3,2],[2,3],[3,2],[0,2],[0,2],[3,0]]]
ZW = 518
def setup_inputs(rng):
    return {"z": rng.standard_normal((N, 128, ZW), dtype=np.float32), "g": rng.random((N, 128, T * K), dtype=np.float32)}
def reference(z, g):
    y = np.zeros((N, 128, T), np.float64)
    fill = [0] * N
    for r in range(N):
        for t in range(T):
            for k, e in enumerate(ROUTE[r][t]):
                y[r][:, t] += g[r][:, t * K + k].astype(np.float64) * z[e][:, fill[e]].astype(np.float64)
                fill[e] += 1
    return {"y": y.astype(z.dtype)}

@@ -1,0 +1,96 @@
+from concourse.mybir import AluOpType
+
+_N = 4
+_LANDW = 256
+
+SCRATCH = {
+    "zs": ("sbuf", [128, 520], "float32"),
+    "gs": ("sbuf", [128, 512], "float32"),
+    "prod": ("sbuf", [128, 512], "float32"),
+    "ys": ("sbuf", [128, 256], "float32"),
+    "land0": ("sbuf", [128, _LANDW], "float32"),
+    "land1": ("sbuf", [128, _LANDW], "float32"),
+    "land2": ("sbuf", [128, _LANDW], "float32"),
+    "land3": ("sbuf", [128, _LANDW], "float32"),
+}
+SEMAPHORES = ["zl", "gl", "sent", "arr0", "arr1", "arr2", "arr3", "mul", "added", "stored"]
+
+
+def _plan(route, n, k_per):
+    cols = [[[] for _ in range(n)] for _ in range(n)]
+    for r in range(n):
+        for t, experts in enumerate(route[r]):
+            for k, e in enumerate(experts):
+                cols[e][r].append(t * k_per + k)
+    return cols
+
+
+def _runs(c):
+    out = []
+    i, n = 0, len(c)
+    while i < n:
+        if i == n - 1:
+            out.append((i, 1, 1))
+            break
+        d = c[i + 1] - c[i]
+        j = i + 1
+        while j + 1 < n and c[j + 1] - c[j] == d:
+            j += 1
+        out.append((i, j - i + 1, d))
+        i = j + 1
+    return out
+
+
+def rank_program(g, core, T, topo):
+    r = T.rank_of(core)
+    if r is None:
+        return
+    n = len(T.cores)
+    k_per = T.tables["K"]
+    tokens = T.tables["T"]
+    cols = _plan(T.tables["ROUTE"], n, k_per)
+    cnt = [[len(cols[e][s]) for s in range(n)] for e in range(n)]
+    off = [[sum(cnt[e][:s]) for s in range(n)] for e in range(n)]
+    used = sum(cnt[r])
+    S = T.sem
+
+    g.sync.dma_start(T.zs[:, 0:used], T.z[:, 0:used]).then_inc(S.zl, 16)
+    g.scalar.dma_start(T.gs[:], T.g[:]).then_inc(S.gl, 16)
+
+    g.wait_ge(S.zl, 16)
+    for step in range(1, n):
+        d = (r + step) % n
+        dst = T.cores[d]
+        rid, pid, _se = topo.addr(dst)
+        g.remote_dma(
+            T["land%d" % r][:, 0:cnt[r][d]],
+            T.zs[:, off[r][d]:off[r][d] + cnt[r][d]],
+            S["arr%d" % r], S.sent, pid, rid, topo.mask(core, dst),
+        )
+
+    v = g.vector
+    v.wait_ge(S.gl, 16)
+    v.wait_ge(S.zl, 16)
+    nmul = 0
+    for step in range(n):
+        e = (r - step) % n
+        if e == r:
+            src, base = T.zs, off[r][r]
+        else:
+            src, base = T["land%d" % e], 0
+            v.wait_ge(S["arr%d" % e], 16)
+        c = cols[e][r]
+        for (j, ln, d) in _runs(c):
+            lo, hi = c[j], c[j + ln - 1] + 1
+            v.tensor_tensor(T.prod[:, lo:hi:d], T.gs[:, lo:hi:d], src[:, base + j:base + j + ln],
+                            AluOpType.mult).then_inc(S.mul, 1)
+            nmul += 1
+
+    v.wait_ge(S.mul, nmul)
+    v.tensor_tensor(T.ys[:], T.prod[:, 0:k_per * tokens:k_per], T.prod[:, 1:k_per * tokens:k_per],
+                    AluOpType.add).then_inc(S.added, 1)
+    g.sync.wait_ge(S.added, 1)
+    g.sync.dma_start(T.y[:], T.ys[:]).then_inc(S.stored, 16)
+    g.sync.wait_ge(S.stored, 16)
+
+    g.wait_ge(S.sent, 16 * (n - 1))

@@ -1,6 +1,5 @@
 from concourse.mybir import AluOpType
 
-_N = 4
 _LANDW = 256
 
 SCRATCH = {
@@ -26,18 +25,27 @@ def _plan(route, n, k_per):
 
 
 def _runs(c):
+    n = len(c)
+    left = set(range(n))
     out = []
-    i, n = 0, len(c)
-    while i < n:
-        if i == n - 1:
-            out.append((i, 1, 1))
-            break
-        d = c[i + 1] - c[i]
-        j = i + 1
-        while j + 1 < n and c[j + 1] - c[j] == d:
-            j += 1
-        out.append((i, j - i + 1, d))
-        i = j + 1
+    while left:
+        best = (1, min(left), 1, 1)
+        for i in sorted(left):
+            for a in range(1, n - i):
+                if (n - 1 - i) // a + 1 <= best[0]:
+                    break
+                if i + a not in left:
+                    continue
+                b = c[i + a] - c[i]
+                ln = 2
+                while i + a * ln in left and c[i + a * ln] - c[i + a * (ln - 1)] == b:
+                    ln += 1
+                if ln > best[0]:
+                    best = (ln, i, a, b)
+        ln, i, a, b = best
+        out.append((i, ln, a, b))
+        for q in range(ln):
+            left.discard(i + a * q)
     return out
 
 
@@ -80,9 +88,10 @@ def rank_program(g, core, T, topo):
             src, base = T["land%d" % e], 0
             v.wait_ge(S["arr%d" % e], 16)
         c = cols[e][r]
-        for (j, ln, d) in _runs(c):
-            lo, hi = c[j], c[j + ln - 1] + 1
-            v.tensor_tensor(T.prod[:, lo:hi:d], T.gs[:, lo:hi:d], src[:, base + j:base + j + ln],
+        for (j, ln, a, b) in _runs(c):
+            lo, hi = c[j], c[j] + (ln - 1) * b + 1
+            jlo, jhi = base + j, base + j + (ln - 1) * a + 1
+            v.tensor_tensor(T.prod[:, lo:hi:b], T.gs[:, lo:hi:b], src[:, jlo:jhi:a],
                             AluOpType.mult).then_inc(S.mul, 1)
             nmul += 1
 

from concourse.mybir import AluOpType

_LANDW = 256

SCRATCH = {
    "zs": ("sbuf", [128, 520], "float32"),
    "gs": ("sbuf", [128, 512], "float32"),
    "prod": ("sbuf", [128, 512], "float32"),
    "ys": ("sbuf", [128, 256], "float32"),
    "land0": ("sbuf", [128, _LANDW], "float32"),
    "land1": ("sbuf", [128, _LANDW], "float32"),
    "land2": ("sbuf", [128, _LANDW], "float32"),
    "land3": ("sbuf", [128, _LANDW], "float32"),
}
SEMAPHORES = ["zl", "gl", "sent", "arr0", "arr1", "arr2", "arr3", "mul", "added", "stored"]


def _plan(route, n, k_per):
    cols = [[[] for _ in range(n)] for _ in range(n)]
    for r in range(n):
        for t, experts in enumerate(route[r]):
            for k, e in enumerate(experts):
                cols[e][r].append(t * k_per + k)
    return cols


def _runs(c):
    n = len(c)
    left = set(range(n))
    out = []
    while left:
        best = (1, min(left), 1, 1)
        for i in sorted(left):
            for a in range(1, n - i):
                if (n - 1 - i) // a + 1 <= best[0]:
                    break
                if i + a not in left:
                    continue
                b = c[i + a] - c[i]
                ln = 2
                while i + a * ln in left and c[i + a * ln] - c[i + a * (ln - 1)] == b:
                    ln += 1
                if ln > best[0]:
                    best = (ln, i, a, b)
        ln, i, a, b = best
        out.append((i, ln, a, b))
        for q in range(ln):
            left.discard(i + a * q)
    return out


def rank_program(g, core, T, topo):
    r = T.rank_of(core)
    if r is None:
        return
    n = len(T.cores)
    k_per = T.tables["K"]
    tokens = T.tables["T"]
    cols = _plan(T.tables["ROUTE"], n, k_per)
    cnt = [[len(cols[e][s]) for s in range(n)] for e in range(n)]
    off = [[sum(cnt[e][:s]) for s in range(n)] for e in range(n)]
    used = sum(cnt[r])
    S = T.sem

    g.sync.dma_start(T.zs[:, 0:used], T.z[:, 0:used]).then_inc(S.zl, 16)
    g.scalar.dma_start(T.gs[:], T.g[:]).then_inc(S.gl, 16)

    g.wait_ge(S.zl, 16)
    for step in range(1, n):
        d = (r + step) % n
        dst = T.cores[d]
        rid, pid, _se = topo.addr(dst)
        g.remote_dma(
            T["land%d" % r][:, 0:cnt[r][d]],
            T.zs[:, off[r][d]:off[r][d] + cnt[r][d]],
            S["arr%d" % r], S.sent, pid, rid, topo.mask(core, dst),
        )

    v = g.vector
    v.wait_ge(S.gl, 16)
    v.wait_ge(S.zl, 16)
    nmul = 0
    for step in range(n):
        e = (r - step) % n
        if e == r:
            src, base = T.zs, off[r][r]
        else:
            src, base = T["land%d" % e], 0
            v.wait_ge(S["arr%d" % e], 16)
        c = cols[e][r]
        for (j, ln, a, b) in _runs(c):
            lo, hi = c[j], c[j] + (ln - 1) * b + 1
            jlo, jhi = base + j, base + j + (ln - 1) * a + 1
            v.tensor_tensor(T.prod[:, lo:hi:b], T.gs[:, lo:hi:b], src[:, jlo:jhi:a],
                            AluOpType.mult).then_inc(S.mul, 1)
            nmul += 1

    v.wait_ge(S.mul, nmul)
    v.tensor_tensor(T.ys[:], T.prod[:, 0:k_per * tokens:k_per], T.prod[:, 1:k_per * tokens:k_per],
                    AluOpType.add).then_inc(S.added, 1)
    g.sync.wait_ge(S.added, 1)
    g.sync.dma_start(T.y[:], T.ys[:]).then_inc(S.stored, 16)
    g.sync.wait_ge(S.stored, 16)

    g.wait_ge(S.sent, 16 * (n - 1))
